import numpy as np
import ml_dtypes


def mxq(x, axis, fmt="e4m3"):
    dtype, down = {"e4m3": (ml_dtypes.float8_e4m3fn, 7), "e5m2": (ml_dtypes.float8_e5m2, 14)}[fmt]
    v = np.moveaxis(np.asarray(x, np.float32).astype(ml_dtypes.bfloat16).astype(np.float64), axis, -1)
    blocks = v.reshape(v.shape[:-1] + (-1, 32))
    amax = np.abs(blocks).max(-1, keepdims=True)
    byte = np.maximum(np.where(amax > 0, np.frexp(amax)[1] - 1 + 127, 0) - down, 1)
    scale = np.exp2(byte - 127.0)
    codes = (blocks / scale).astype(np.float32).astype(dtype).astype(np.float64)
    return np.moveaxis((codes * scale).reshape(v.shape), -1, axis)


WIDE = False


def mx_kscale(k):
    if not WIDE:
        return np.ones(k)
    levels = np.array([10, -10, 5, -5, 0])
    if k % 512:
        return np.exp2(np.random.permutation(np.resize(levels, k // 32))).repeat(32)
    a = np.empty((k // 512, 16))
    for p in range(k // 512):
        a[p, :8] = np.random.permutation(np.resize(levels, 8))
        for g in range(8):
            far = levels[np.abs(levels - a[p, g]) >= 10]
            a[p, g + 8] = far[np.random.randint(len(far))]
    return np.exp2(a.ravel()).repeat(32)


def f64(x):
    return np.asarray(x).astype(np.float64)


def striped(idx):
    return np.tile(np.asarray(idx).reshape(-1, 16).T, (8, 1)).astype(np.uint16)


def unstriped(offs):
    return offs[:16].T.reshape(-1).astype(np.int64)


E2M1 = np.array([0.0, 0.5, 1.0, 1.5, 2.0, 3.0, 4.0, 6.0, -0.0, -0.5, -1.0, -1.5, -2.0, -3.0, -4.0, -6.0])


def pack_weight(w, fmt):
    k, n = w.shape
    w = f64(np.asarray(w, np.float32).astype(ml_dtypes.bfloat16)).reshape(k // 32, 32, n)
    amax = np.abs(w).max(1)
    if fmt == "e4m3":
        byte = np.frexp(amax)[1] - 1 + 127 - 7
    else:
        mant, ex = np.frexp(amax / 6.0)
        byte = np.where(mant > 0.5, ex, ex - 1) + 127
    byte = np.clip(np.where(amax > 0, byte, 1), 1, 254)
    scaled = (w * np.exp2(127.0 - byte)[:, None, :]).reshape(k, n).astype(np.float32)
    by_word = np.ascontiguousarray(scaled.reshape(k // 512, 128, 4, n).transpose(0, 1, 3, 2))
    if fmt == "e4m3":
        words = by_word.astype(ml_dtypes.float8_e4m3fn).view(np.uint8)
    else:
        c = by_word.astype(ml_dtypes.float4_e2m1fn).view(np.uint8) & 0xF
        words = (c[..., 0::2] | (c[..., 1::2] << 4)).reshape(k // 512, 128, 2 * n)
    return np.ascontiguousarray(words), np.ascontiguousarray(byte.astype(np.uint8).reshape(k // 512, 16, n))


def unpack_weight(words, scales, fmt):
    g, _, n = scales.shape
    words = np.ascontiguousarray(words).reshape(g, 128, n, -1)
    if fmt == "e4m3":
        vals = words.view(ml_dtypes.float8_e4m3fn).astype(np.float64)
    else:
        nib = np.empty((g, 128, n, 4), np.uint8)
        nib[..., 0::2] = words & 0xF
        nib[..., 1::2] = words >> 4
        vals = E2M1[nib]
    vals = vals * np.repeat(np.exp2(scales.astype(np.float64) - 127.0), 8, axis=1)[..., None]
    return vals.transpose(0, 1, 3, 2).reshape(g * 512, n)


def bf(x):
    return np.asarray(x, np.float32).astype(ml_dtypes.bfloat16)


def planes(Y):
    r, m = Y.shape
    b = f64(bf(Y)).reshape(r // 32, 32, m)
    amax = np.abs(b).max(1)
    byte = np.clip(np.where(amax > 0, np.frexp(amax)[1] - 1 + 127 - 7, 1), 1, 254)
    codes = (b * np.exp2(127.0 - byte)[:, None, :]).reshape(r, m).astype(np.float32).astype(ml_dtypes.float8_e4m3fn).view(np.uint8)
    words = codes.reshape(r // 512, 128, 4, m).transpose(0, 1, 3, 2)
    return np.ascontiguousarray(words), np.ascontiguousarray(byte.astype(np.uint8).reshape(r // 512, 16, m))


D, T, I, Q, E = 512, 2048, 512, 256, 512


def setup_inputs():
    n = np.random.standard_normal
    idx = np.random.permutation(T)[:I]
    fd = mx_kscale(D)
    fi = mx_kscale(I)
    ti = np.ones(T)
    ti[idx] = fi
    keysp = pack_weight(n((D, T)) / fd[:, None], "e2m1")
    return {
        "query": (n((D, Q)) * 0.6 / np.sqrt(D) * fd[:, None]).astype(np.float32),
        "keys_words": keysp[0],
        "keys_scales": keysp[1],
        "level": (np.random.uniform(0.5, 0.9, (Q, 1))).astype(np.float32),
        "size": (np.random.uniform(0.5, 2.0, (1, I)) * fi).astype(np.float32),
        "vals": (n((E, T)) / ti).astype(np.float32),
        "offs": striped(idx),
    }


def reference(query, keys_words, keys_scales, level, size, vals, offs):
    idx = unstriped(offs)
    keysu = unpack_weight(keys_words, keys_scales, "e2m1")
    queryq = mxq(f64(query), 0, "e4m3")
    keysidxg = keysu[:, idx]
    a = queryq.T @ keysidxg
    p = np.exp(a - np.max(a, axis=1, keepdims=True))
    r = np.maximum(p / np.sum(p, axis=1, keepdims=True) * 512.0 - f64(level), 0.0)
    w = r * f64(size) / np.sum(r, axis=1, keepdims=True)
    wt = w.T
    vt = f64(vals)[:, idx].T
    vtq = mxq(vt, 0, "e4m3")
    wtq = mxq(wt, 0, "e4m3")
    o = vtq.T @ wtq
    words, scales = planes(o)
    return o, words, scales

@@ -1,0 +1,166 @@
+from contextlib import ExitStack
+
+import concourse.mybir as mybir
+from concourse.masks import make_identity
+
+D, T, I, Q, E = 512, 2048, 512, 256, 512
+FLOPS = 2 * D * Q * I + 2 * I * E * Q
+
+F32 = mybir.dt.float32
+BF16 = mybir.dt.bfloat16
+I32 = mybir.dt.int32
+U32 = mybir.dt.uint32
+U16 = mybir.dt.uint16
+U8 = mybir.dt.uint8
+FP8X4 = mybir.dt.float8_e4m3fn_x4
+FP4X4 = mybir.dt.float4_e2m1fn_x4
+ALU = mybir.AluOpType
+ACT = mybir.ActivationFunctionType
+AXIS = mybir.AxisListType
+
+P = 128
+PACK = 4
+HALVES = Q // P
+
+
+def tile_attend_sharesabove_pl_kernel(tc, query, keys_words, keys_scales, level, size, vals, offs, out_0, out_1, out_2):
+    nc = tc.nc
+    with ExitStack() as ctx:
+        keep = ctx.enter_context(tc.tile_pool(name="keep", bufs=1))
+        psum = ctx.enter_context(tc.psum_pool(name="psum", bufs=1))
+
+        offsets = keep.tile([P, I // 16], U16, name="offsets")
+        key_pool = keep.tile([P, T], U16, name="key_pool", align_bytes=64)
+        key_scale_pool = keep.tile([P, T], U8, name="key_scale_pool", align_bytes=64)
+        query_rows = keep.tile([P, PACK, Q], F32, name="query_rows")
+        small_rows = keep.tile([P, P], F32, name="small_rows")
+        value_pools = [keep.tile([P, T], F32, name=f"value_pool{j}") for j in range(PACK)]
+        identity = keep.tile([P, P], F32, name="identity")
+        warm_in = keep.tile([P, 1], F32, name="warm_in")
+        warm_out = keep.tile([P, 1], F32, name="warm_out")
+
+        nc.vector.memset(key_scale_pool[:].bitcast(I32), 0)
+        nc.vector.memset(warm_in[:], 0.0)
+        nc.gpsimd.memset(small_rows[:], 0.0)
+
+        nc.sync.dma_start(offsets[:], offs)
+        nc.sync.dma_start(key_pool[:].bitcast(I32), keys_words[0].bitcast(I32))
+        for quad in range(4):
+            nc.sync.dma_start(
+                key_scale_pool[32 * quad : 32 * quad + 4, :].bitcast(I32),
+                keys_scales[0, 4 * quad : 4 * quad + 4, :].bitcast(I32),
+            )
+        nc.sync.dma_start(small_rows[0:PACK, :], size[0].rearrange("(r c) -> r c", c=P))
+        nc.sync.dma_start(small_rows[PACK : PACK + HALVES, :], level.rearrange("(h p) o -> h (p o)", p=P))
+        nc.sync.dma_start(query_rows[:], query.rearrange("(p j) q -> p j q", j=PACK))
+        value_rows = vals.rearrange("(p j) t -> j p t", j=PACK)
+        for j in range(PACK):
+            nc.sync.dma_start(value_pools[j][:], value_rows[j])
+        make_identity(nc, identity[:])
+        nc.scalar.activation(warm_out[:], warm_in[:], ACT.Exp)
+
+        key_words = keep.tile([P, I], U16, name="key_words", align_bytes=64)
+        key_scales = keep.tile([P, I], U8, name="key_scales", align_bytes=64)
+        nc.vector.tensor_copy(key_words[:], key_pool[:].indirect(offsets[:]))
+        nc.vector.tensor_copy(key_scales[:], key_scale_pool[:].indirect(offsets[:]))
+
+        scores = []
+        for h in range(HALVES):
+            grouped = keep.tile([P, P, PACK], BF16, name=f"query_grouped{h}", align_bytes=64)
+            nc.scalar.copy(grouped[:], query_rows[:, :, h * P : (h + 1) * P].rearrange("p j q -> p q j"))
+            codes = keep.tile([P, P], U32, name=f"query_codes{h}", align_bytes=64)
+            scales = keep.tile([P, P], U8, name=f"query_scales{h}", align_bytes=64)
+            nc.vector.quantize_mx(codes[:].bitcast(FP8X4), scales[:], grouped[:].rearrange("p q j -> p (q j)"))
+            bank = psum.tile([P, I], F32, name=f"scores{h}", tag=f"row_bank{h}")
+            nc.tensor.matmul_mx(
+                bank[:], lhsT=codes[:].bitcast(FP8X4), lhsT_scale=scales[:],
+                rhs=key_words[:].bitcast(FP4X4), rhs_scale=key_scales[:], start=True, stop=True,
+            )
+            scores.append(bank)
+
+        small_turned = psum.tile([P, P], F32, name="small_turned", tag="turn_bank1")
+        nc.tensor.transpose(small_turned[:], small_rows[:], identity[:])
+        size_cols = keep.tile([P, PACK], F32, name="size_cols")
+        nc.scalar.copy(size_cols[:], small_turned[:, 0:PACK])
+        level_step = keep.tile([P, HALVES], F32, name="level_step")
+        nc.scalar.activation(level_step[:], small_turned[:, PACK : PACK + HALVES], ACT.Copy, scale=-1.0 / I)
+        size_bank = psum.tile([P, PACK, P], F32, name="size_bank")
+        for r in range(PACK):
+            nc.tensor.transpose(size_bank[:, r, :], size_cols[:, r : r + 1].to_broadcast([P, P]), identity[:])
+
+        weight_grouped = keep.tile([P, HALVES, P, PACK], BF16, name="weight_grouped", tag="reuse2", align_bytes=64)
+        for h in range(HALVES):
+            neg_max = keep.tile([P, 1], F32, name=f"neg_max{h}", tag=("reuse0" if h == 0 else "neg_max1"), align_bytes=64)
+            nc.vector.tensor_reduce(neg_max[:], scores[h][:], AXIS.X, ALU.max, negate=True)
+            shares = keep.tile([P, I], F32, name=f"shares{h}")
+            share_sum = keep.tile([P, 1], F32, name=f"share_sum{h}")
+            nc.scalar.activation(shares[:], scores[h][:], ACT.Exp, bias=neg_max[:], accum_out=share_sum[:])
+            neg_bar = keep.tile([P, 1], F32, name=f"neg_bar{h}")
+            nc.scalar.activation(neg_bar[:], share_sum[:], ACT.Copy, scale=level_step[:, h : h + 1])
+            excess = keep.tile([P, I], F32, name=f"excess{h}", tag=("reuse1" if h == 1 else "excess0"), align_bytes=64)
+            excess_sum = keep.tile([P, 1], F32, name=f"excess_sum{h}")
+            nc.scalar.activation(excess[:], shares[:], ACT.Relu, bias=neg_bar[:], accum_out=excess_sum[:])
+            inv_sum = keep.tile([P, 1], F32, name=f"inv_sum{h}")
+            nc.vector.reciprocal(inv_sum[:], excess_sum[:])
+            weights = keep.tile([P, I], BF16, name=f"weights{h}", align_bytes=64)
+            nc.vector.scalar_tensor_tensor(
+                weights[:], excess[:], inv_sum[:], size_bank[:].rearrange("p r c -> p (r c)"),
+                ALU.mult, ALU.mult,
+            )
+            turned = psum.tile([P, 2, P], F32, name=f"weights_turned{h}", tag=f"row_bank{h}")
+            pairs = weights[:].bitcast(F32)
+            for u in range(2):
+                nc.tensor.transpose(turned[:, u, :], pairs[:, u : 2 * P : 2], identity[:])
+            nc.scalar.copy(
+                weight_grouped[:, h].rearrange("p q t -> p (q t)").bitcast(F32).rearrange("p (q u) -> p q u", u=2),
+                turned[:].rearrange("p u q -> p q u"),
+            )
+        weight_codes = keep.tile([P, Q], U32, name="weight_codes", align_bytes=64)
+        weight_scales = keep.tile([P, Q], U8, name="weight_scales", align_bytes=64)
+        nc.vector.quantize_mx(
+            weight_codes[:].bitcast(FP8X4), weight_scales[:], weight_grouped[:].rearrange("p h q t -> p (h q t)")
+        )
+
+        sums = [psum.tile([P, PACK, P], F32, name=f"sums{h}") for h in range(HALVES)]
+        early = keep.tile([P, PACK - 1, Q], F32, name="early")
+        last = keep.tile([P, Q], F32, name="last")
+        out_rows = out_0.rearrange("(p j) q -> p j q", j=PACK)
+        for j in range(PACK):
+            picked = keep.tile([P, I], BF16, name=f"picked{j}", tag=f"reuse{j}", align_bytes=64)
+            nc.vector.tensor_copy(picked[:], value_pools[j][:].indirect(offsets[:]))
+            turned = psum.tile([P, 2, P], F32, name=f"values_turned{j}", tag=f"turn_bank{j % 2}")
+            pairs = picked[:].bitcast(F32)
+            for u in range(2):
+                nc.tensor.transpose(turned[:, u, :], pairs[:, u : 2 * P : 2], identity[:])
+            grouped = keep.tile([P, P * PACK], BF16, name=f"value_grouped{j}", tag=("reuse3" if j == 2 else f"value_grouped{j}"), align_bytes=64)
+            nc.scalar.copy(grouped[:].bitcast(F32).rearrange("p (e u) -> p e u", u=2), turned[:].rearrange("p u e -> p e u"))
+            codes = keep.tile([P, P], U32, name=f"value_codes{j}", align_bytes=64)
+            scales = keep.tile([P, P], U8, name=f"value_scales{j}", align_bytes=64)
+            nc.vector.quantize_mx(codes[:].bitcast(FP8X4), scales[:], grouped[:])
+            for h in range(HALVES):
+                cols = slice(h * P, (h + 1) * P)
+                nc.tensor.matmul_mx(
+                    sums[h][:, j, :], lhsT=codes[:].bitcast(FP8X4), lhsT_scale=scales[:],
+                    rhs=weight_codes[:, cols].bitcast(FP8X4), rhs_scale=weight_scales[:, cols], start=True, stop=True,
+                )
+            if j < PACK - 1:
+                for h in range(HALVES):
+                    nc.scalar.copy(early[:, j, h * P : (h + 1) * P], sums[h][:, j, :])
+        nc.sync.dma_start(out_rows[:, 0 : PACK - 1, :], early[:])
+
+        out_grouped = keep.tile([P, HALVES, P, PACK], BF16, name="out_grouped", align_bytes=64)
+        nc.vector.tensor_copy(out_grouped[:, 0], sums[0][:].rearrange("p j q -> p q j"))
+        nc.scalar.copy(out_grouped[:, 1], sums[1][:].rearrange("p j q -> p q j"))
+        out_codes = keep.tile([P, Q], U32, name="out_codes", align_bytes=64)
+        out_scales = keep.tile([P, Q], U8, name="out_scales", align_bytes=64)
+        nc.vector.quantize_mx(out_codes[:].bitcast(FP8X4), out_scales[:], out_grouped[:].rearrange("p h q t -> p (h q t)"))
+        for h in reversed(range(HALVES)):
+            nc.scalar.copy(last[:, h * P : (h + 1) * P], sums[h][:, PACK - 1, :])
+        nc.scalar.dma_start(out_rows[:, PACK - 1, :], last[:])
+        nc.sync.dma_start(out_1[0].rearrange("p c r -> p (c r)").bitcast(I32), out_codes[:].bitcast(I32))
+        for quad in range(4):
+            queue = nc.sync if quad < 2 else nc.scalar
+            queue.dma_start(
+                out_2[0, 4 * quad : 4 * quad + 4, :].bitcast(I32),
+                out_scales[32 * quad : 32 * quad + 4, :].bitcast(I32),
+            )

@@ -34,25 +34,25 @@ def tile_attend_sharesabove_pl_kernel(tc, query, keys_words, keys_scales, level,
         key_scale_pool = keep.tile([P, T], U8, name="key_scale_pool", align_bytes=64)
         query_rows = keep.tile([P, PACK, Q], F32, name="query_rows")
         small_rows = keep.tile([P, P], F32, name="small_rows")
-        value_pools = [keep.tile([P, T], F32, name=f"value_pool{j}") for j in range(PACK)]
+        value_pools = [keep.tile([P, T], F32, name=f"value_pool{j}", tag=f"value_pool{j}", align_bytes=64) for j in range(PACK)]
         identity = keep.tile([P, P], F32, name="identity")
         warm_in = keep.tile([P, 1], F32, name="warm_in")
         warm_out = keep.tile([P, 1], F32, name="warm_out")
 
-        nc.vector.memset(key_scale_pool[:].bitcast(I32), 0)
+        nc.gpsimd.memset(key_scale_pool[:].bitcast(I32), 0)
         nc.vector.memset(warm_in[:], 0.0)
         nc.gpsimd.memset(small_rows[:], 0.0)
 
-        nc.sync.dma_start(offsets[:], offs)
         nc.sync.dma_start(key_pool[:].bitcast(I32), keys_words[0].bitcast(I32))
+        nc.sync.dma_start(offsets[:], offs)
         for quad in range(4):
             nc.sync.dma_start(
                 key_scale_pool[32 * quad : 32 * quad + 4, :].bitcast(I32),
                 keys_scales[0, 4 * quad : 4 * quad + 4, :].bitcast(I32),
             )
+        nc.sync.dma_start(query_rows[:], query.rearrange("(p j) q -> p j q", j=PACK))
         nc.sync.dma_start(small_rows[0:PACK, :], size[0].rearrange("(r c) -> r c", c=P))
         nc.sync.dma_start(small_rows[PACK : PACK + HALVES, :], level.rearrange("(h p) o -> h (p o)", p=P))
-        nc.sync.dma_start(query_rows[:], query.rearrange("(p j) q -> p j q", j=PACK))
         value_rows = vals.rearrange("(p j) t -> j p t", j=PACK)
         for j in range(PACK):
             nc.sync.dma_start(value_pools[j][:], value_rows[j])
@@ -68,8 +68,8 @@ def tile_attend_sharesabove_pl_kernel(tc, query, keys_words, keys_scales, level,
         for h in range(HALVES):
             grouped = keep.tile([P, P, PACK], BF16, name=f"query_grouped{h}", align_bytes=64)
             nc.scalar.copy(grouped[:], query_rows[:, :, h * P : (h + 1) * P].rearrange("p j q -> p q j"))
-            codes = keep.tile([P, P], U32, name=f"query_codes{h}", align_bytes=64)
-            scales = keep.tile([P, P], U8, name=f"query_scales{h}", align_bytes=64)
+            codes = keep.tile([P, P], U32, name=f"query_codes{h}", tag=f"query_codes{h}", align_bytes=64)
+            scales = keep.tile([P, P], U8, name=f"query_scales{h}", tag=f"query_scales{h}", align_bytes=64)
             nc.vector.quantize_mx(codes[:].bitcast(FP8X4), scales[:], grouped[:].rearrange("p q j -> p (q j)"))
             bank = psum.tile([P, I], F32, name=f"scores{h}", tag=f"row_bank{h}")
             nc.tensor.matmul_mx(
@@ -88,24 +88,58 @@ def tile_attend_sharesabove_pl_kernel(tc, query, keys_words, keys_scales, level,
         for r in range(PACK):
             nc.tensor.transpose(size_bank[:, r, :], size_cols[:, r : r + 1].to_broadcast([P, P]), identity[:])
 
-        weight_grouped = keep.tile([P, HALVES, P, PACK], BF16, name="weight_grouped", tag="reuse2", align_bytes=64)
+        def gather_values(j, tag):
+            picked = keep.tile([P, I], BF16, name=f"picked{j}", tag=tag, align_bytes=64)
+            nc.vector.tensor_copy(picked[:], value_pools[j][:].indirect(offsets[:]))
+            turned = psum.tile([P, 2, P], F32, name=f"values_turned{j}", tag=f"turn_bank{j % 2}")
+            pairs = picked[:].bitcast(F32)
+            for u in range(2):
+                nc.tensor.transpose(turned[:, u, :], pairs[:, u : 2 * P : 2], identity[:])
+            return turned
+
+        def group_values(j, turned, tag):
+            grouped = keep.tile([P, P * PACK], BF16, name=f"value_grouped{j}", tag=tag, align_bytes=64)
+            nc.scalar.copy(grouped[:].bitcast(F32).rearrange("p (e u) -> p e u", u=2), turned[:].rearrange("p u e -> p e u"))
+            return grouped
+
+        def quantise_values(j, grouped, tag):
+            codes = keep.tile([P, P], U32, name=f"value_codes{j}", tag=tag, align_bytes=64)
+            scales = keep.tile([P, P], U8, name=f"value_scales{j}", align_bytes=64)
+            nc.vector.quantize_mx(codes[:].bitcast(FP8X4), scales[:], grouped[:])
+            return codes, scales
+
+        def multiply(j, codes, scales):
+            for h in range(HALVES):
+                cols = slice(h * P, (h + 1) * P)
+                nc.tensor.matmul_mx(
+                    sums[h][:, j, :], lhsT=codes[:].bitcast(FP8X4), lhsT_scale=scales[:],
+                    rhs=weight_codes[:, cols].bitcast(FP8X4), rhs_scale=weight_scales[:, cols], start=True, stop=True,
+                )
+
+        neg_max, excess = [], []
+        excess_sums = keep.tile([P, HALVES], F32, name="excess_sums")
         for h in range(HALVES):
-            neg_max = keep.tile([P, 1], F32, name=f"neg_max{h}", tag=("reuse0" if h == 0 else "neg_max1"), align_bytes=64)
-            nc.vector.tensor_reduce(neg_max[:], scores[h][:], AXIS.X, ALU.max, negate=True)
-            shares = keep.tile([P, I], F32, name=f"shares{h}")
+            neg_max.append(keep.tile([P, 1], F32, name=f"neg_max{h}"))
+            nc.vector.tensor_reduce(neg_max[h][:], scores[h][:], AXIS.X, ALU.max, negate=True)
+        for h in range(HALVES):
+            shares = keep.tile([P, I], F32, name=f"shares{h}", tag=f"shares{h}", align_bytes=64)
             share_sum = keep.tile([P, 1], F32, name=f"share_sum{h}")
-            nc.scalar.activation(shares[:], scores[h][:], ACT.Exp, bias=neg_max[:], accum_out=share_sum[:])
-            neg_bar = keep.tile([P, 1], F32, name=f"neg_bar{h}")
+            nc.scalar.activation(shares[:], scores[h][:], ACT.Exp, bias=neg_max[h][:], accum_out=share_sum[:])
+            neg_bar = keep.tile([P, 1], F32, name=f"neg_bar{h}", tag=f"neg_bar{h}", align_bytes=64)
             nc.scalar.activation(neg_bar[:], share_sum[:], ACT.Copy, scale=level_step[:, h : h + 1])
-            excess = keep.tile([P, I], F32, name=f"excess{h}", tag=("reuse1" if h == 1 else "excess0"), align_bytes=64)
-            excess_sum = keep.tile([P, 1], F32, name=f"excess_sum{h}")
-            nc.scalar.activation(excess[:], shares[:], ACT.Relu, bias=neg_bar[:], accum_out=excess_sum[:])
-            inv_sum = keep.tile([P, 1], F32, name=f"inv_sum{h}")
-            nc.vector.reciprocal(inv_sum[:], excess_sum[:])
+            excess.append(keep.tile([P, I], F32, name=f"excess{h}", tag=f"excess{h}", align_bytes=64))
+            nc.scalar.activation(excess[h][:], shares[:], ACT.Relu, bias=neg_bar[:], accum_out=excess_sums[:, h : h + 1])
+
+        turned0 = gather_values(0, "query_codes1")
+        turned1 = gather_values(1, "query_scales1")
+
+        inv_sums = keep.tile([P, HALVES], F32, name="inv_sums", tag="value_pool1", align_bytes=64)
+        nc.vector.reciprocal(inv_sums[:], excess_sums[:])
+        weight_grouped = keep.tile([P, HALVES, P, PACK], BF16, name="weight_grouped", tag="weight_grouped", align_bytes=64)
+        for h in range(HALVES):
             weights = keep.tile([P, I], BF16, name=f"weights{h}", align_bytes=64)
             nc.vector.scalar_tensor_tensor(
-                weights[:], excess[:], inv_sum[:], size_bank[:].rearrange("p r c -> p (r c)"),
-                ALU.mult, ALU.mult,
+                weights[:], excess[h][:], inv_sums[:, h : h + 1], size_bank[:].rearrange("p r c -> p (r c)"), ALU.mult, ALU.mult
             )
             turned = psum.tile([P, 2, P], F32, name=f"weights_turned{h}", tag=f"row_bank{h}")
             pairs = weights[:].bitcast(F32)
@@ -115,37 +149,29 @@ def tile_attend_sharesabove_pl_kernel(tc, query, keys_words, keys_scales, level,
                 weight_grouped[:, h].rearrange("p q t -> p (q t)").bitcast(F32).rearrange("p (q u) -> p q u", u=2),
                 turned[:].rearrange("p u q -> p q u"),
             )
-        weight_codes = keep.tile([P, Q], U32, name="weight_codes", align_bytes=64)
+        grouped0 = group_values(0, turned0, "shares1")
+        grouped1 = group_values(1, turned1, "neg_bar1")
+        turned2 = gather_values(2, "excess1")
+        weight_codes = keep.tile([P, Q], U32, name="weight_codes", tag="value_pool2", align_bytes=64)
         weight_scales = keep.tile([P, Q], U8, name="weight_scales", align_bytes=64)
         nc.vector.quantize_mx(
             weight_codes[:].bitcast(FP8X4), weight_scales[:], weight_grouped[:].rearrange("p h q t -> p (h q t)")
         )
-
         sums = [psum.tile([P, PACK, P], F32, name=f"sums{h}") for h in range(HALVES)]
         early = keep.tile([P, PACK - 1, Q], F32, name="early")
         last = keep.tile([P, Q], F32, name="last")
         out_rows = out_0.rearrange("(p j) q -> p j q", j=PACK)
-        for j in range(PACK):
-            picked = keep.tile([P, I], BF16, name=f"picked{j}", tag=f"reuse{j}", align_bytes=64)
-            nc.vector.tensor_copy(picked[:], value_pools[j][:].indirect(offsets[:]))
-            turned = psum.tile([P, 2, P], F32, name=f"values_turned{j}", tag=f"turn_bank{j % 2}")
-            pairs = picked[:].bitcast(F32)
-            for u in range(2):
-                nc.tensor.transpose(turned[:, u, :], pairs[:, u : 2 * P : 2], identity[:])
-            grouped = keep.tile([P, P * PACK], BF16, name=f"value_grouped{j}", tag=("reuse3" if j == 2 else f"value_grouped{j}"), align_bytes=64)
-            nc.scalar.copy(grouped[:].bitcast(F32).rearrange("p (e u) -> p e u", u=2), turned[:].rearrange("p u e -> p e u"))
-            codes = keep.tile([P, P], U32, name=f"value_codes{j}", align_bytes=64)
-            scales = keep.tile([P, P], U8, name=f"value_scales{j}", align_bytes=64)
-            nc.vector.quantize_mx(codes[:].bitcast(FP8X4), scales[:], grouped[:])
-            for h in range(HALVES):
-                cols = slice(h * P, (h + 1) * P)
-                nc.tensor.matmul_mx(
-                    sums[h][:, j, :], lhsT=codes[:].bitcast(FP8X4), lhsT_scale=scales[:],
-                    rhs=weight_codes[:, cols].bitcast(FP8X4), rhs_scale=weight_scales[:, cols], start=True, stop=True,
-                )
-            if j < PACK - 1:
-                for h in range(HALVES):
-                    nc.scalar.copy(early[:, j, h * P : (h + 1) * P], sums[h][:, j, :])
+        multiply(0, *quantise_values(0, grouped0, "excess0"))
+        multiply(1, *quantise_values(1, grouped1, "value_codes1"))
+        grouped2 = group_values(2, turned2, "value_grouped2")
+        for h in range(HALVES):
+            nc.scalar.copy(early[:, 0:2, h * P : (h + 1) * P], sums[h][:, 0:2, :])
+        turned3 = gather_values(3, "weight_grouped")
+        multiply(2, *quantise_values(2, grouped2, "value_pool3"))
+        for h in range(HALVES):
+            nc.vector.tensor_copy(early[:, 2, h * P : (h + 1) * P], sums[h][:, 2, :])
+        grouped3 = group_values(3, turned3, "value_grouped3")
+        multiply(3, *quantise_values(3, grouped3, "value_codes3"))
         nc.sync.dma_start(out_rows[:, 0 : PACK - 1, :], early[:])
 
         out_grouped = keep.tile([P, HALVES, P, PACK], BF16, name="out_grouped", align_bytes=64)

@@ -97,24 +97,22 @@ def tile_attend_sharesabove_pl_kernel(tc, query, keys_words, keys_scales, level,
                 nc.tensor.transpose(turned[:, u, :], pairs[:, u : 2 * P : 2], identity[:])
             return turned
 
-        def group_values(j, turned, tag):
-            grouped = keep.tile([P, P * PACK], BF16, name=f"value_grouped{j}", tag=tag, align_bytes=64)
-            nc.scalar.copy(grouped[:].bitcast(F32).rearrange("p (e u) -> p e u", u=2), turned[:].rearrange("p u e -> p e u"))
-            return grouped
+        def group_values(turned, grouped):
+            nc.scalar.copy(grouped.bitcast(F32).rearrange("p (e u) -> p e u", u=2), turned[:].rearrange("p u e -> p e u"))
 
         def quantise_values(j, grouped, tag):
             codes = keep.tile([P, P], U32, name=f"value_codes{j}", tag=tag, align_bytes=64)
             scales = keep.tile([P, P], U8, name=f"value_scales{j}", align_bytes=64)
             nc.vector.quantize_mx(codes[:].bitcast(FP8X4), scales[:], grouped[:])
-            return codes, scales
+            return codes[:], scales[:]
 
-        def multiply(j, codes, scales):
-            for h in range(HALVES):
-                cols = slice(h * P, (h + 1) * P)
-                nc.tensor.matmul_mx(
-                    sums[h][:, j, :], lhsT=codes[:].bitcast(FP8X4), lhsT_scale=scales[:],
-                    rhs=weight_codes[:, cols].bitcast(FP8X4), rhs_scale=weight_scales[:, cols], start=True, stop=True,
-                )
+        def multiply(j, h):
+            cols = slice(h * P, (h + 1) * P)
+            codes, scales = operands[j]
+            nc.tensor.matmul_mx(
+                sums[j // 2][h][:, j % 2, :], lhsT=codes.bitcast(FP8X4), lhsT_scale=scales,
+                rhs=joint_codes[:, cols].bitcast(FP8X4), rhs_scale=joint_scales[:, cols], start=True, stop=True,
+            )
 
         neg_max, excess = [], []
         excess_sums = keep.tile([P, HALVES], F32, name="excess_sums")
@@ -135,7 +133,7 @@ def tile_attend_sharesabove_pl_kernel(tc, query, keys_words, keys_scales, level,
 
         inv_sums = keep.tile([P, HALVES], F32, name="inv_sums", tag="value_pool1", align_bytes=64)
         nc.vector.reciprocal(inv_sums[:], excess_sums[:])
-        weight_grouped = keep.tile([P, HALVES, P, PACK], BF16, name="weight_grouped", tag="weight_grouped", align_bytes=64)
+        joint_grouped = keep.tile([P, HALVES + 2, P * PACK], BF16, name="joint_grouped", tag="shares1", align_bytes=64)
         for h in range(HALVES):
             weights = keep.tile([P, I], BF16, name=f"weights{h}", align_bytes=64)
             nc.vector.scalar_tensor_tensor(
@@ -146,43 +144,49 @@ def tile_attend_sharesabove_pl_kernel(tc, query, keys_words, keys_scales, level,
             for u in range(2):
                 nc.tensor.transpose(turned[:, u, :], pairs[:, u : 2 * P : 2], identity[:])
             nc.scalar.copy(
-                weight_grouped[:, h].rearrange("p q t -> p (q t)").bitcast(F32).rearrange("p (q u) -> p q u", u=2),
+                joint_grouped[:, h].bitcast(F32).rearrange("p (q u) -> p q u", u=2),
                 turned[:].rearrange("p u q -> p q u"),
             )
-        grouped0 = group_values(0, turned0, "shares1")
-        grouped1 = group_values(1, turned1, "neg_bar1")
-        turned2 = gather_values(2, "excess1")
-        weight_codes = keep.tile([P, Q], U32, name="weight_codes", tag="value_pool2", align_bytes=64)
-        weight_scales = keep.tile([P, Q], U8, name="weight_scales", align_bytes=64)
-        nc.vector.quantize_mx(
-            weight_codes[:].bitcast(FP8X4), weight_scales[:], weight_grouped[:].rearrange("p h q t -> p (h q t)")
-        )
-        sums = [psum.tile([P, PACK, P], F32, name=f"sums{h}") for h in range(HALVES)]
-        early = keep.tile([P, PACK - 1, Q], F32, name="early")
-        last = keep.tile([P, Q], F32, name="last")
-        out_rows = out_0.rearrange("(p j) q -> p j q", j=PACK)
-        multiply(0, *quantise_values(0, grouped0, "excess0"))
-        multiply(1, *quantise_values(1, grouped1, "value_codes1"))
-        grouped2 = group_values(2, turned2, "value_grouped2")
+        group_values(turned0, joint_grouped[:, HALVES])
+        group_values(turned1, joint_grouped[:, HALVES + 1])
+        turned2 = gather_values(2, "picked2")
+        grouped2 = keep.tile([P, P * PACK], BF16, name="value_grouped2", align_bytes=64)
+        group_values(turned2, grouped2[:])
+        turned3 = gather_values(3, "picked3")
+        joint_codes = keep.tile([P, (HALVES + 2) * P], U32, name="joint_codes", tag="value_pool3", align_bytes=64)
+        joint_scales = keep.tile([P, (HALVES + 2) * P], U8, name="joint_scales", align_bytes=64)
+        nc.vector.quantize_mx(joint_codes[:].bitcast(FP8X4), joint_scales[:], joint_grouped[:].rearrange("p a c -> p (a c)"))
+        operands = [(joint_codes[:, Q + j * P : Q + (j + 1) * P], joint_scales[:, Q + j * P : Q + (j + 1) * P]) for j in range(2)]
+        operands.append(quantise_values(2, grouped2, "shares1"))
+        grouped3 = keep.tile([P, P * PACK], BF16, name="value_grouped3", align_bytes=64)
+        group_values(turned3, grouped3[:])
+        operands.append(quantise_values(3, grouped3, "value_codes3"))
+        sums = [
+            [psum.tile([P, 2, P], F32, name=f"sums{u}{h}", tag=(f"row_bank{h}" if u == 0 else f"sum_bank{h}")) for h in range(HALVES)]
+            for u in range(2)
+        ]
+        results = [keep.tile([P, 2, Q], F32, name=f"results{u}") for u in range(2)]
+        out_rows = out_0.rearrange("(p u e) q -> p u e q", u=2, e=2)
+        out_grouped = keep.tile([P, Q, 2, 2], BF16, name="out_grouped", align_bytes=64)
+        halves = [slice(h * P, (h + 1) * P) for h in range(HALVES)]
         for h in range(HALVES):
-            nc.scalar.copy(early[:, 0:2, h * P : (h + 1) * P], sums[h][:, 0:2, :])
-        turned3 = gather_values(3, "weight_grouped")
-        multiply(2, *quantise_values(2, grouped2, "value_pool3"))
+            multiply(0, h)
+            multiply(1, h)
+            nc.scalar.copy(results[0][:, :, halves[h]], sums[0][h][:])
+        for j in (2, 3):
+            for h in range(HALVES):
+                multiply(j, h)
+        nc.sync.dma_start(out_rows[:, 0], results[0][:])
         for h in range(HALVES):
-            nc.vector.tensor_copy(early[:, 2, h * P : (h + 1) * P], sums[h][:, 2, :])
-        grouped3 = group_values(3, turned3, "value_grouped3")
-        multiply(3, *quantise_values(3, grouped3, "value_codes3"))
-        nc.sync.dma_start(out_rows[:, 0 : PACK - 1, :], early[:])
-
-        out_grouped = keep.tile([P, HALVES, P, PACK], BF16, name="out_grouped", align_bytes=64)
-        nc.vector.tensor_copy(out_grouped[:, 0], sums[0][:].rearrange("p j q -> p q j"))
-        nc.scalar.copy(out_grouped[:, 1], sums[1][:].rearrange("p j q -> p q j"))
+            nc.vector.tensor_copy(out_grouped[:, halves[h], 0, :], results[0][:, :, halves[h]].rearrange("p e q -> p q e"))
+        nc.vector.tensor_copy(out_grouped[:, halves[0], 1, :], sums[1][0][:].rearrange("p e q -> p q e"))
+        nc.scalar.copy(out_grouped[:, halves[1], 1, :], sums[1][1][:].rearrange("p e q -> p q e"))
         out_codes = keep.tile([P, Q], U32, name="out_codes", align_bytes=64)
         out_scales = keep.tile([P, Q], U8, name="out_scales", align_bytes=64)
-        nc.vector.quantize_mx(out_codes[:].bitcast(FP8X4), out_scales[:], out_grouped[:].rearrange("p h q t -> p (h q t)"))
+        nc.vector.quantize_mx(out_codes[:].bitcast(FP8X4), out_scales[:], out_grouped[:].rearrange("p q u e -> p (q u e)"))
         for h in reversed(range(HALVES)):
-            nc.scalar.copy(last[:, h * P : (h + 1) * P], sums[h][:, PACK - 1, :])
-        nc.scalar.dma_start(out_rows[:, PACK - 1, :], last[:])
+            nc.scalar.copy(results[1][:, :, halves[h]], sums[1][h][:])
+        nc.scalar.dma_start(out_rows[:, 1], results[1][:])
         nc.sync.dma_start(out_1[0].rearrange("p c r -> p (c r)").bitcast(I32), out_codes[:].bitcast(I32))
         for quad in range(4):
             queue = nc.sync if quad < 2 else nc.scalar

from contextlib import ExitStack

import concourse.mybir as mybir
from concourse.masks import make_identity

D, T, I, Q, E = 512, 2048, 512, 256, 512
FLOPS = 2 * D * Q * I + 2 * I * E * Q

F32 = mybir.dt.float32
BF16 = mybir.dt.bfloat16
I32 = mybir.dt.int32
U32 = mybir.dt.uint32
U16 = mybir.dt.uint16
U8 = mybir.dt.uint8
FP8X4 = mybir.dt.float8_e4m3fn_x4
FP4X4 = mybir.dt.float4_e2m1fn_x4
ALU = mybir.AluOpType
ACT = mybir.ActivationFunctionType
AXIS = mybir.AxisListType

P = 128
PACK = 4
HALVES = Q // P


def tile_attend_sharesabove_pl_kernel(tc, query, keys_words, keys_scales, level, size, vals, offs, out_0, out_1, out_2):
    nc = tc.nc
    with ExitStack() as ctx:
        keep = ctx.enter_context(tc.tile_pool(name="keep", bufs=1))
        psum = ctx.enter_context(tc.psum_pool(name="psum", bufs=1))

        offsets = keep.tile([P, I // 16], U16, name="offsets")
        key_pool = keep.tile([P, T], U16, name="key_pool", align_bytes=64)
        key_scale_pool = keep.tile([P, T], U8, name="key_scale_pool", align_bytes=64)
        query_rows = keep.tile([P, PACK, Q], F32, name="query_rows")
        small_rows = keep.tile([P, P], F32, name="small_rows")
        value_pools = [keep.tile([P, T], F32, name=f"value_pool{j}", tag=f"value_pool{j}", align_bytes=64) for j in range(PACK)]
        identity = keep.tile([P, P], F32, name="identity")
        warm_in = keep.tile([P, 1], F32, name="warm_in")
        warm_out = keep.tile([P, 1], F32, name="warm_out")

        nc.gpsimd.memset(key_scale_pool[:].bitcast(I32), 0)
        nc.vector.memset(warm_in[:], 0.0)
        nc.gpsimd.memset(small_rows[:], 0.0)

        nc.sync.dma_start(key_pool[:].bitcast(I32), keys_words[0].bitcast(I32))
        nc.sync.dma_start(offsets[:], offs)
        for quad in range(4):
            nc.sync.dma_start(
                key_scale_pool[32 * quad : 32 * quad + 4, :].bitcast(I32),
                keys_scales[0, 4 * quad : 4 * quad + 4, :].bitcast(I32),
            )
        nc.sync.dma_start(query_rows[:], query.rearrange("(p j) q -> p j q", j=PACK))
        nc.sync.dma_start(small_rows[0:PACK, :], size[0].rearrange("(r c) -> r c", c=P))
        nc.sync.dma_start(small_rows[PACK : PACK + HALVES, :], level.rearrange("(h p) o -> h (p o)", p=P))
        value_rows = vals.rearrange("(p j) t -> j p t", j=PACK)
        for j in range(PACK):
            nc.sync.dma_start(value_pools[j][:], value_rows[j])
        make_identity(nc, identity[:])
        nc.scalar.activation(warm_out[:], warm_in[:], ACT.Exp)

        key_words = keep.tile([P, I], U16, name="key_words", align_bytes=64)
        key_scales = keep.tile([P, I], U8, name="key_scales", align_bytes=64)
        nc.vector.tensor_copy(key_words[:], key_pool[:].indirect(offsets[:]))
        nc.vector.tensor_copy(key_scales[:], key_scale_pool[:].indirect(offsets[:]))

        scores = []
        for h in range(HALVES):
            grouped = keep.tile([P, P, PACK], BF16, name=f"query_grouped{h}", align_bytes=64)
            nc.scalar.copy(grouped[:], query_rows[:, :, h * P : (h + 1) * P].rearrange("p j q -> p q j"))
            codes = keep.tile([P, P], U32, name=f"query_codes{h}", tag=f"query_codes{h}", align_bytes=64)
            scales = keep.tile([P, P], U8, name=f"query_scales{h}", tag=f"query_scales{h}", align_bytes=64)
            nc.vector.quantize_mx(codes[:].bitcast(FP8X4), scales[:], grouped[:].rearrange("p q j -> p (q j)"))
            bank = psum.tile([P, I], F32, name=f"scores{h}", tag=f"row_bank{h}")
            nc.tensor.matmul_mx(
                bank[:], lhsT=codes[:].bitcast(FP8X4), lhsT_scale=scales[:],
                rhs=key_words[:].bitcast(FP4X4), rhs_scale=key_scales[:], start=True, stop=True,
            )
            scores.append(bank)

        small_turned = psum.tile([P, P], F32, name="small_turned", tag="turn_bank1")
        nc.tensor.transpose(small_turned[:], small_rows[:], identity[:])
        size_cols = keep.tile([P, PACK], F32, name="size_cols")
        nc.scalar.copy(size_cols[:], small_turned[:, 0:PACK])
        level_step = keep.tile([P, HALVES], F32, name="level_step")
        nc.scalar.activation(level_step[:], small_turned[:, PACK : PACK + HALVES], ACT.Copy, scale=-1.0 / I)
        size_bank = psum.tile([P, PACK, P], F32, name="size_bank")
        for r in range(PACK):
            nc.tensor.transpose(size_bank[:, r, :], size_cols[:, r : r + 1].to_broadcast([P, P]), identity[:])

        def gather_values(j, tag):
            picked = keep.tile([P, I], BF16, name=f"picked{j}", tag=tag, align_bytes=64)
            nc.vector.tensor_copy(picked[:], value_pools[j][:].indirect(offsets[:]))
            turned = psum.tile([P, 2, P], F32, name=f"values_turned{j}", tag=f"turn_bank{j % 2}")
            pairs = picked[:].bitcast(F32)
            for u in range(2):
                nc.tensor.transpose(turned[:, u, :], pairs[:, u : 2 * P : 2], identity[:])
            return turned

        def group_values(turned, grouped):
            nc.scalar.copy(grouped.bitcast(F32).rearrange("p (e u) -> p e u", u=2), turned[:].rearrange("p u e -> p e u"))

        def quantise_values(j, grouped, tag):
            codes = keep.tile([P, P], U32, name=f"value_codes{j}", tag=tag, align_bytes=64)
            scales = keep.tile([P, P], U8, name=f"value_scales{j}", align_bytes=64)
            nc.vector.quantize_mx(codes[:].bitcast(FP8X4), scales[:], grouped[:])
            return codes[:], scales[:]

        def multiply(j, h):
            cols = slice(h * P, (h + 1) * P)
            codes, scales = operands[j]
            nc.tensor.matmul_mx(
                sums[j // 2][h][:, j % 2, :], lhsT=codes.bitcast(FP8X4), lhsT_scale=scales,
                rhs=joint_codes[:, cols].bitcast(FP8X4), rhs_scale=joint_scales[:, cols], start=True, stop=True,
            )

        neg_max, excess = [], []
        excess_sums = keep.tile([P, HALVES], F32, name="excess_sums")
        for h in range(HALVES):
            neg_max.append(keep.tile([P, 1], F32, name=f"neg_max{h}"))
            nc.vector.tensor_reduce(neg_max[h][:], scores[h][:], AXIS.X, ALU.max, negate=True)
        for h in range(HALVES):
            shares = keep.tile([P, I], F32, name=f"shares{h}", tag=f"shares{h}", align_bytes=64)
            share_sum = keep.tile([P, 1], F32, name=f"share_sum{h}")
            nc.scalar.activation(shares[:], scores[h][:], ACT.Exp, bias=neg_max[h][:], accum_out=share_sum[:])
            neg_bar = keep.tile([P, 1], F32, name=f"neg_bar{h}", tag=f"neg_bar{h}", align_bytes=64)
            nc.scalar.activation(neg_bar[:], share_sum[:], ACT.Copy, scale=level_step[:, h : h + 1])
            excess.append(keep.tile([P, I], F32, name=f"excess{h}", tag=f"excess{h}", align_bytes=64))
            nc.scalar.activation(excess[h][:], shares[:], ACT.Relu, bias=neg_bar[:], accum_out=excess_sums[:, h : h + 1])

        turned0 = gather_values(0, "query_codes1")
        turned1 = gather_values(1, "query_scales1")

        inv_sums = keep.tile([P, HALVES], F32, name="inv_sums", tag="value_pool1", align_bytes=64)
        nc.vector.reciprocal(inv_sums[:], excess_sums[:])
        joint_grouped = keep.tile([P, HALVES + 2, P * PACK], BF16, name="joint_grouped", tag="shares1", align_bytes=64)
        for h in range(HALVES):
            weights = keep.tile([P, I], BF16, name=f"weights{h}", align_bytes=64)
            nc.vector.scalar_tensor_tensor(
                weights[:], excess[h][:], inv_sums[:, h : h + 1], size_bank[:].rearrange("p r c -> p (r c)"), ALU.mult, ALU.mult
            )
            turned = psum.tile([P, 2, P], F32, name=f"weights_turned{h}", tag=f"row_bank{h}")
            pairs = weights[:].bitcast(F32)
            for u in range(2):
                nc.tensor.transpose(turned[:, u, :], pairs[:, u : 2 * P : 2], identity[:])
            nc.scalar.copy(
                joint_grouped[:, h].bitcast(F32).rearrange("p (q u) -> p q u", u=2),
                turned[:].rearrange("p u q -> p q u"),
            )
        group_values(turned0, joint_grouped[:, HALVES])
        group_values(turned1, joint_grouped[:, HALVES + 1])
        turned2 = gather_values(2, "picked2")
        grouped2 = keep.tile([P, P * PACK], BF16, name="value_grouped2", align_bytes=64)
        group_values(turned2, grouped2[:])
        turned3 = gather_values(3, "picked3")
        joint_codes = keep.tile([P, (HALVES + 2) * P], U32, name="joint_codes", tag="value_pool3", align_bytes=64)
        joint_scales = keep.tile([P, (HALVES + 2) * P], U8, name="joint_scales", align_bytes=64)
        nc.vector.quantize_mx(joint_codes[:].bitcast(FP8X4), joint_scales[:], joint_grouped[:].rearrange("p a c -> p (a c)"))
        operands = [(joint_codes[:, Q + j * P : Q + (j + 1) * P], joint_scales[:, Q + j * P : Q + (j + 1) * P]) for j in range(2)]
        operands.append(quantise_values(2, grouped2, "shares1"))
        grouped3 = keep.tile([P, P * PACK], BF16, name="value_grouped3", align_bytes=64)
        group_values(turned3, grouped3[:])
        operands.append(quantise_values(3, grouped3, "value_codes3"))
        sums = [
            [psum.tile([P, 2, P], F32, name=f"sums{u}{h}", tag=(f"row_bank{h}" if u == 0 else f"sum_bank{h}")) for h in range(HALVES)]
            for u in range(2)
        ]
        results = [keep.tile([P, 2, Q], F32, name=f"results{u}") for u in range(2)]
        out_rows = out_0.rearrange("(p u e) q -> p u e q", u=2, e=2)
        out_grouped = keep.tile([P, Q, 2, 2], BF16, name="out_grouped", align_bytes=64)
        halves = [slice(h * P, (h + 1) * P) for h in range(HALVES)]
        for h in range(HALVES):
            multiply(0, h)
            multiply(1, h)
            nc.scalar.copy(results[0][:, :, halves[h]], sums[0][h][:])
        for j in (2, 3):
            for h in range(HALVES):
                multiply(j, h)
        nc.sync.dma_start(out_rows[:, 0], results[0][:])
        for h in range(HALVES):
            nc.vector.tensor_copy(out_grouped[:, halves[h], 0, :], results[0][:, :, halves[h]].rearrange("p e q -> p q e"))
        nc.vector.tensor_copy(out_grouped[:, halves[0], 1, :], sums[1][0][:].rearrange("p e q -> p q e"))
        nc.scalar.copy(out_grouped[:, halves[1], 1, :], sums[1][1][:].rearrange("p e q -> p q e"))
        out_codes = keep.tile([P, Q], U32, name="out_codes", align_bytes=64)
        out_scales = keep.tile([P, Q], U8, name="out_scales", align_bytes=64)
        nc.vector.quantize_mx(out_codes[:].bitcast(FP8X4), out_scales[:], out_grouped[:].rearrange("p q u e -> p (q u e)"))
        for h in reversed(range(HALVES)):
            nc.scalar.copy(results[1][:, :, halves[h]], sums[1][h][:])
        nc.scalar.dma_start(out_rows[:, 1], results[1][:])
        nc.sync.dma_start(out_1[0].rearrange("p c r -> p (c r)").bitcast(I32), out_codes[:].bitcast(I32))
        for quad in range(4):
            queue = nc.sync if quad < 2 else nc.scalar
            queue.dma_start(
                out_2[0, 4 * quad : 4 * quad + 4, :].bitcast(I32),
                out_scales[32 * quad : 32 * quad + 4, :].bitcast(I32),
            )
